import numpy as np
CORES = [40,64,80,88,96,104,120,144]
N = 8
HOST = [c // 128 for c in CORES]
HS = sorted(set(HOST)); H = len(HS)
R, T = 8192, 1024
def entries(a): return a.T.reshape(-1)
def pack(v, P): return np.ascontiguousarray(np.asarray(v, np.int32).reshape(-1, P).T)
def lists(rng, how):
    A = np.array(HOST); L = [rng.permutation(N * R)[:T] for h in HS]
    if how == "away": L = [R * int(rng.choice(np.flatnonzero(A != h))) + rng.permutation(R)[:T] for h in HS]
    if how == "edge": E = R * np.arange(N); E = np.concatenate([E, E + R - 1]); F = np.setdiff1d(np.arange(N * R), E); L = [rng.permutation(np.concatenate([E, rng.permutation(F)[:T - 2 * N]])) for h in HS]
    if how == "home": O = np.repeat(A, R); L = [rng.permutation(np.flatnonzero(O == h))[:T] for h in HS]
    if how == "hotrank": z = R * int(rng.integers(N)); L = [z + rng.permutation(R)[:T] for h in HS]
    if how == "meet": L = [rng.permutation(L[0]) for h in HS]
    return {"idx": np.stack([pack(L[HS.index(HOST[r])], 16) for r in range(N)])}
def setup_inputs(rng):
    return dict({"g": rng.standard_normal((N, 128, T), dtype=np.float32)}, **lists(rng, "uniform"))
def setup_inputs_away(rng):
    d = setup_inputs(rng); d.update(lists(rng, "away"))
    for k in ("g",): d[k] = (d[k].astype(np.float32) * 1024.0).astype(d[k].dtype)
    return d
def setup_inputs_edge(rng):
    d = setup_inputs(rng); d.update(lists(rng, "edge"))
    for k in ("g",): d[k] = (d[k].astype(np.float32) * (1 / 1024.0)).astype(d[k].dtype)
    return d
def setup_inputs_home(rng):
    d = setup_inputs(rng); d.update(lists(rng, "home"))
    return d
def setup_inputs_hotrank(rng):
    d = setup_inputs(rng); d.update(lists(rng, "hotrank"))
    return d
def setup_inputs_meet(rng):
    d = setup_inputs(rng); d.update(lists(rng, "meet"))
    return d
def check_inputs(x):
    bad = []
    if x["idx"].min() < 0 or x["idx"].max() >= N * R: bad.append("idx out of range")
    if any(len(np.unique(a)) != a.size for a in x["idx"]): bad.append("a number stands twice in a list")
    if any(HOST[p] == HOST[s] and not np.array_equal(x["idx"][p], x["idx"][s]) for p in range(N) for s in range(p)): bad.append("two ranks of one host hold different lists")
    return bad
def reference(g, idx):
    S = np.zeros((128, N * R))
    for q in range(N):
        I = entries(idx[q]); S[:, I] += g[q].astype(np.float64)
    return {"y": np.stack([S[:, R * r:R * r + R] for r in range(N)]).astype(np.float32)}

from concourse.bass import DstId, RemoteDMATransfer
from concourse.mybir import AluOpType as Alu, ActivationFunctionType as Act

R, TT = 8192, 1024
NQ, NJ = 4, 8
PAD = 1136
WW = TT + 2 * PAD
GW = 2 * TT + 4
PARTS = ((0, 128), (128, 512))
BLOCKS = (512, 512, 1024, 1024, 1024, 1024, 1024, 1024, 512, 512)
F, I, U, H = "float32", "int32", "uint16", "float16"
SCRATCH = {
    "gd": ("dram", [4096, 32], F),
    "ga": ("dram", [4096, 32], F),
    "gb": ("dram", [4096, 32], F),
    "rel": ("dram", [1024, 32], F),
    "inb": ("dram", [896, 32], F),
    "g1b": ("dram", [128, 32], F),
    "ixd": ("dram", [128, 8], I),
    "ixo": ("dram", [128, 8], I),
    "ix": ("sbuf", [128, 64], I), "iy": ("sbuf", [128, 64], I),
    "key0": ("sbuf", [128, 64], I), "key1": ("sbuf", [128, 64], I),
    "nm0": ("sbuf", [128, 64], I), "nm1": ("sbuf", [128, 64], I),
    "u0": ("sbuf", [128, 64], I), "u1": ("sbuf", [128, 64], I),
    "b0": ("sbuf", [128, 64], I), "b1": ("sbuf", [128, 64], I),
    "w0": ("sbuf", [128, 64], I), "w1": ("sbuf", [128, 64], I),
    "o0": ("sbuf", [128, 64], U), "o1": ("sbuf", [128, 64], U),
    "d0": ("sbuf", [128, 64], I), "d1": ("sbuf", [128, 64], I),
    "pn": ("sbuf", [128, 1], I), "pg": ("sbuf", [128, 1], I), "kp": ("sbuf", [128, 1], F),
    "ve": ("sbuf", [128, TT], F),
    "win0": ("sbuf", [128, WW], F), "win1": ("sbuf", [128, WW], F),
    "f0": ("sbuf", [128, TT], H), "f1": ("sbuf", [128, TT], H),
    "rw": ("sbuf", [128, TT], F),
    "zz": ("sbuf", [128, 143], F),
    "one": ("sbuf", [128, 128], F), "la": ("sbuf", [128, 128], F), "lb": ("sbuf", [128, 128], F),
    "l0": ("sbuf", [128, 128], F), "l1": ("sbuf", [128, 128], F),
    "h0": ("sbuf", [128, 128], H), "h1": ("sbuf", [128, 128], H),
    "p0s": ("sbuf", [128, 512], F), "ofm": ("sbuf", [128, 512], F), "off": ("sbuf", [128, 512], U),
    "mo": ("sbuf", [128, 64], U),
    "gcat": ("sbuf", [128, GW], F), "lt": ("sbuf", [128, TT], F), "yt": ("sbuf", [128, R], F),
    "pm": ("psum", [128, 512], F), "p0": ("psum", [128, 512], F),
    "pa": ("psum", [128, 512], F), "pb": ("psum", [128, 512], F),
}
NE = 90
SEMAPHORES = ["h1a", "rs", "rg", "aa", "ab", "xi", "sent"] + ["e%d" % k for k in range(NE)]


def slot(t, s):
    return t[128 * s:128 * s + 128, :]


def engines(topo, src, dsts):
    m = 0xFFFF
    for d in dsts:
        m &= topo.mask(src, d)
    return [b for b in range(16) if m >> b & 1]


def bits(es):
    m = 0
    for b in es:
        m |= 1 << b
    return m


def dst(topo, d, s):
    rid, pid = topo.addr(d, s)
    return DstId(rid=rid, pnc=pid)


def same_chip(topo, a, b):
    return topo.host(a) == topo.host(b) and topo.chip(a) == topo.chip(b)


def helpers(T, topo, r):
    me, base = T.cores[r], T.cores[r] - T.cores[r] % 8
    hs = [c for c in range(base, base + 8) if c != me and same_chip(topo, c, me)
          and all(topo.may_write(c, d) for d in T.cores)]
    a = [c for c in hs if topo.die(c) == topo.die(me)]
    b = [c for c in hs if topo.die(c) != topo.die(me)]
    return [c for ab in zip(a, b) for c in ab][:NQ]


def list_plan(T, topo, home):
    n = len(T.cores)
    far = [r for r in range(n) if topo.host(T.cores[r]) != home]
    own = [r for r in range(n) if topo.host(T.cores[r]) == home]
    reach = {r: [d for d in far if topo.may_write(T.cores[r], T.cores[d])] for r in own}
    lead = max(own, key=lambda r: (len(reach[r]), -r))
    rest = [d for d in far if d not in reach[lead]]
    return lead, reach[lead], rest, (helpers(T, topo, lead)[0] if rest else None)


def rank_program(g, core, T, topo):
    cores = T.cores
    n = len(cores)
    by = {}
    for r in range(n):
        by.setdefault(topo.host(cores[r]), []).append(r)
    many = max(by.values(), key=len)
    lone = [r for r in range(n) if r not in many][0]
    H4 = [helpers(T, topo, r) for r in range(n)]
    lists = [list_plan(T, topo, h) for h in by]
    if T.rank_of(core) is not None:
        rank_core(g, core, T, topo, many, lone, H4, lists)
        return
    for i in range(n):
        if core in H4[i]:
            helper_core(g, core, T, topo, many, lone, H4, lists, i, H4[i].index(core))


def send_list(g, core, T, topo, src, targets):
    e = engines(topo, core, targets)[:1]
    g.remote_dma_fused([RemoteDMATransfer(dst_ids=[dst(topo, d, core) for d in targets], dma_engine_mask=bits(e),
                                          remote_sem=T.sem.xi, srcs=[src], dsts=[T.ixo[:] for d in targets], alu_op=0)],
                       local_sem=T.sem.sent)
    return 1


def helper_core(g, core, T, topo, many, lone, H4, lists, i, h):
    cores, n, sent = T.cores, len(T.cores), 0
    for lead, near, rest, relay in lists:
        if relay == core:
            g.wait_ge(T.sem.xi, 1)
            sent += send_list(g, core, T, topo, T.ixo[:], [cores[d] for d in rest])
    g.wait_ge(T.sem.h1a, NJ)
    js = [j for j in range(n) if j != i]
    es = engines(topo, core, [H4[j][h] for j in js])
    tr = []
    for k, j in enumerate(js):
        to, sem = (T.g1b[:], T.sem.rg) if i == lone else (slot(T.inb, many.index(i)), T.sem.rs)
        tr.append(RemoteDMATransfer(dst_ids=[dst(topo, H4[j][h], core)], dma_engine_mask=bits([es[k]]), remote_sem=sem,
                                    srcs=[slot(T.rel, j)], dsts=[to], alu_op=0))
    g.remote_dma_fused(tr, local_sem=T.sem.sent)
    sent += len(tr)
    s, ds = NJ * h + i, [cores[r] for r in many]
    es = engines(topo, core, cores)
    if i == lone:
        src = slot(T.rel, i)
    else:
        g.wait_ge(T.sem.rg, 1)
        src = T.g1b[:]
    g.remote_dma_fused([RemoteDMATransfer(dst_ids=[dst(topo, d, core) for d in ds], dma_engine_mask=bits(es),
                                          remote_sem=T.sem.ab, srcs=[src], dsts=[slot(T.gb, s) for d in ds], alu_op=0)],
                       local_sem=T.sem.sent)
    sent += len(es)
    others = [r for r in many if r != i]
    g.wait_ge(T.sem.rs, len(others))
    srcs = [slot(T.inb, many.index(r)) for r in others] + ([slot(T.rel, i)] if i in many else [])
    g.remote_dma_fused([RemoteDMATransfer(dst_ids=[dst(topo, d, core) for d in cores], dma_engine_mask=bits(es),
                                          remote_sem=T.sem.aa, srcs=srcs, dsts=[slot(T.ga, s) for d in cores], alu_op=1)],
                       local_sem=T.sem.sent)
    sent += len(es)
    g.wait_ge(T.sem.sent, sent)


def rank_core(g, core, T, topo, many, lone, H4, lists):
    r = T.rank_of(core)
    cores, n, sent = T.cores, len(T.cores), 0
    v, s, sy, pe = g.vector, g.scalar, g.sync, g.tensor
    used, waited = [0], {}

    def ev():
        used[0] += 1
        return used[0] - 1

    def need(q, e, val=1):
        waited[e] = True
        q.wait_ge(T.sem["e%d" % e], val)

    def do(ins, val=1, e=None):
        k = ev() if e is None else e
        ins.then_inc(T.sem["e%d" % k], val)
        return k

    lead = [p for p in lists if p[0] == r]
    if lead:
        e_ixd = do(s.dma_start(out=T.ixd[:], in_=T.idx[:]), 16)
    e_ga = do(sy.dma_start(out=T.gd[0:2048, :], in_=T.g[0:64, :]), 16)
    e_gb = do(sy.dma_start(out=T.gd[2048:4096, :], in_=T.g[64:128, :]), 16)
    e_ix = ev()
    for k in range(8):
        q = s if k < 5 else sy
        do(q.dma_start(out=T.ix[16 * k:16 * k + 16, :], in_=T.idx[:]), 16, e_ix)
    if r == lone:
        e_E = do(sy.dma_start(out=T.gcat[:, TT:2 * TT], in_=T.g[:]), 16)

    e_pn = do(g.iota(T.pn[:], [[0, 1]], 0, 1))
    e_d0 = do(g.iota(T.d0[:], [[16, 64]], TT, 1))
    e_d1 = do(g.iota(T.d1[:], [[16, 64]], TT + PAD, 1))
    e_v0 = do(g.iota(T.ve[:, 0:256], [[1, 256]], TT, 0, allow_small_or_imprecise_dtypes=True))
    for ld, near, rest, relay in lead:
        need(g, e_ixd, 16)
        sent += send_list(g, core, T, topo, T.ixd[:], [cores[d] for d in near] + ([relay] if rest else []))
    for half, e_half in ((0, e_ga), (1, e_gb)):
        need(g, e_half, 16)
        hs = (2 * half, 2 * half + 1)
        es = engines(topo, core, [H4[r][h] for h in hs])
        tr = []
        for j in range(NJ):
            for h in hs:
                tr.append(RemoteDMATransfer(dst_ids=[dst(topo, H4[r][h], core)], dma_engine_mask=bits([es[len(tr)]]),
                                            remote_sem=T.sem.h1a, srcs=[slot(T.gd, NJ * h + j)],
                                            dsts=[slot(T.rel, j)], alu_op=0))
        g.remote_dma_fused(tr, local_sem=T.sem.sent)
        sent += len(tr)

    e_w0 = do(v.memset(T.win0[:, 0:TT], 2048.0))
    e_w0z = do(v.memset(T.win0[:, TT + PAD:WW], 0.0))
    e_one = do(v.memset(T.one[:], 1.0 / 16))
    e_zz = do(v.memset(T.zz[:], 0.0))
    need(v, e_pn)
    e_pg = do(v.tensor_scalar(T.pg[:], T.pn[:], 4, None, Alu.logical_shift_right))
    need(v, e_zz)
    e_zz = do(v.memset(T.zz[:, 15:143:16], 1.0 / 16))
    need(v, e_pg)
    e_kp = do(v.tensor_scalar(T.kp[:], T.pg[:], float(R * r), None, Alu.add))
    e_w1 = do(v.memset(T.win1[:, 0:TT], 3072.0))
    e_zc = do(v.memset(T.gcat[:, 2 * TT:GW], 0.0))

    need(g, e_one)
    e_la = do(g.affine_select(T.la[:], T.one[:], [[0, 8], [0, 2], [-16, 8]], Alu.is_ge, 0.0, 0, 1))
    need(g, e_la)
    e_lb = do(g.affine_select(T.lb[:], T.la[:], [[0, 8], [0, 2], [16, 8]], Alu.is_ge, 0.0, 15, -1))
    need(g, e_lb)
    e_l0 = do(g.affine_select(T.l0[:], T.lb[:], [[0, 8], [-1, 2], [0, 8]], Alu.is_ge, 0.0, 0, 0))
    e_l1 = do(g.affine_select(T.l1[:], T.lb[:], [[0, 8], [1, 2], [0, 8]], Alu.is_ge, 0.0, -1, 0))

    need(s, e_v0)
    e_v1 = do(s.activation(out=T.ve[:, 256:512], in_=T.ve[:, 0:256], func=Act.Copy, bias=256.0))
    need(s, e_v1)
    e_v2 = do(s.activation(out=T.ve[:, 512:1024], in_=T.ve[:, 0:512], func=Act.Copy, bias=512.0))

    def offsets(src, e_src, key, nm, u, b, w, o, d, e_d):
        need(v, e_src, 128)
        a = do(v.tensor_scalar(key[:], src[:], 8 * R - R + 7, None, Alu.bitwise_and))
        e_u = do(v.tensor_scalar(u[:], src[:], 3, TT - 1, Alu.logical_shift_right, Alu.bitwise_and))
        need(v, a)
        a = do(v.tensor_scalar(nm[:], key[:], T.kp[:, 0:1], None, Alu.not_equal))
        need(v, a)
        need(v, e_d)
        a = do(v.tensor_tensor(b[:], nm[:], d[:], Alu.mult))
        need(v, a)
        need(v, e_u)
        a = do(v.tensor_tensor(w[:], u[:], b[:], Alu.max))
        need(v, a)
        return do(v.tensor_copy(out=o[:], in_=w[:]))

    need(v, e_kp)
    e_o0 = offsets(T.ix, e_ix, T.key0, T.nm0, T.u0, T.b0, T.w0, T.o0, T.d0, e_d0)
    for e in (e_o0, e_w0, e_w0z, e_v1, e_v2):
        need(v, e)
    e_s0 = do(v.tensor_copy(out=T.win0[:].indirect(T.o0[:, 0:64]), in_=T.ve[:]))
    need(v, e_l0)
    e_h0 = do(v.tensor_copy(out=T.h0[:], in_=T.l0[:]))
    need(v, e_l1)
    e_h1 = do(v.tensor_copy(out=T.h1[:], in_=T.l1[:]))
    need(v, e_s0)
    e_f0 = do(v.tensor_copy(out=T.f0[:], in_=T.win0[:, 0:TT]))
    for e in (e_h0, e_h1, e_f0):
        need(pe, e)
    pe.matmul(T.p0[:], T.h0[:], T.f0[:, 0:TT:2], True, False)
    e_p0 = do(pe.matmul(T.p0[:], T.h1[:], T.f0[:, 1:TT:2], False, True))

    e_iy = ev()
    for q, ks in ((s, range(0, 4)), (sy, range(4, 8))):
        q.wait_ge(T.sem.xi, 1)
        for k in ks:
            do(q.dma_start(out=T.iy[16 * k:16 * k + 16, :], in_=T.ixo[:]), 16, e_iy)
    need(s, e_p0)
    e_p0s = do(s.activation(out=T.p0s[:], in_=T.p0[:], func=Act.Copy))
    e_o1 = offsets(T.iy, e_iy, T.key1, T.nm1, T.u1, T.b1, T.w1, T.o1, T.d1, e_d1)
    need(s, e_o1)
    need(s, e_s0)
    e_rw = do(s.activation(out=T.rw[:], in_=T.win0[:].indirect(T.o1[:, 0:64]), func=Act.Copy))
    need(pe, e_rw)
    need(pe, e_zz)
    for q in range(16):
        ins = pe.matmul(T.pm[:, 0:64], T.zz[:, 15 - q:143 - q], T.rw[:, q:TT:16], q == 0, q == 15)
    e_pm = do(ins)
    need(v, e_o1)
    need(v, e_w1)
    e_s1 = do(v.tensor_copy(out=T.win1[:].indirect(T.o1[:, 0:64]), in_=T.ve[:]))
    need(v, e_s1)
    e_p1 = []
    for (a, b), ps in zip(PARTS, (T.pa, T.pb)):
        e = do(v.tensor_scalar(T.f1[:, 2 * a:2 * b], T.win1[:, 2 * a:2 * b], -1024.0, None, Alu.add))
        need(pe, e)
        pe.matmul(ps[:, 0:b - a], T.h0[:], T.f1[:, 2 * a:2 * b:2], True, False)
        e_p1.append(do(pe.matmul(ps[:, 0:b - a], T.h1[:], T.f1[:, 2 * a + 1:2 * b:2], False, True)))
    need(v, e_pm)
    e_mo = do(v.tensor_scalar(T.mo[:], T.pm[:, 0:64], -1024.0, 0.0, Alu.add, Alu.max))
    need(v, e_p0s)
    e_off = []
    for (a, b), ps, e in zip(PARTS, (T.pa, T.pb), e_p1):
        need(v, e)
        e = do(v.tensor_tensor(T.ofm[:, a:b], ps[:, 0:b - a], T.p0s[:, a:b], Alu.min))
        need(v, e)
        e_off.append(do(v.tensor_copy(out=T.off[:, a:b], in_=T.ofm[:, a:b])))

    cnt = len(engines(topo, H4[0][0], cores)) * NQ * NJ
    if r == lone:
        sy.wait_ge(T.sem.aa, cnt)
        e_L = do(sy.dma_start(out=T.lt[:], in_=T.ga[:]), 16)
    else:
        sy.wait_ge(T.sem.ab, cnt)
        e_L = do(sy.dma_start(out=T.lt[:], in_=T.gb[:]), 16)
        sy.wait_ge(T.sem.aa, cnt)
        e_E = do(sy.dma_start(out=T.gcat[:, TT:2 * TT], in_=T.ga[:]), 16)
    for e, k in ((e_mo, 1), (e_zc, 1), (e_L, 16), (e_E, 16)):
        need(v, e, k)
    e_ml = do(v.tensor_tensor(T.gcat[:, 0:TT], T.gcat[:, TT:GW].indirect(T.mo[:, 0:64]), T.lt[:], Alu.add))

    for q in (v, s):
        for e, k in ((e_ml, 1), (e_E, 16), (e_zc, 1), (e_off[0], 1), (e_off[1], 1)):
            need(q, e, k)
    e_st, c = ev(), 0
    for k, wd in enumerate(BLOCKS):
        offs = T.off[:, c // 16:(c + wd) // 16]
        if k % 2 == 0:
            e = do(v.tensor_copy(out=T.yt[:, c:c + wd], in_=T.gcat[:].indirect(offs)))
        else:
            e = do(s.activation(out=T.yt[:, c:c + wd], in_=T.gcat[:].indirect(offs), func=Act.Copy))
        need(sy, e)
        do(sy.dma_start(out=T.y[:, c:c + wd], in_=T.yt[:, c:c + wd]), 16, e_st)
        c += wd
    need(sy, e_st, 16 * len(BLOCKS))
    g.wait_ge(T.sem.sent, sent)
    for e in range(used[0]):
        assert e in waited
